import numpy as np
import ml_dtypes


def mxq(x, axis, fmt="e4m3"):
    dtype, down = {"e4m3": (ml_dtypes.float8_e4m3fn, 7), "e5m2": (ml_dtypes.float8_e5m2, 14)}[fmt]
    v = np.moveaxis(np.asarray(x, np.float32).astype(ml_dtypes.bfloat16).astype(np.float64), axis, -1)
    blocks = v.reshape(v.shape[:-1] + (-1, 32))
    amax = np.abs(blocks).max(-1, keepdims=True)
    byte = np.maximum(np.where(amax > 0, np.frexp(amax)[1] - 1 + 127, 0) - down, 1)
    scale = np.exp2(byte - 127.0)
    codes = (blocks / scale).astype(np.float32).astype(dtype).astype(np.float64)
    return np.moveaxis((codes * scale).reshape(v.shape), -1, axis)


WIDE = False


def mx_kscale(k, group=512):
    if not WIDE:
        return np.ones(k)
    levels = np.array([10, -10, 5, -5, 0])
    if group != 512:
        return np.exp2(np.random.permutation(np.resize(levels, k // group))).repeat(group)
    if k % 512:
        return np.exp2(np.random.permutation(np.resize(levels, k // 32))).repeat(32)
    a = np.empty((k // 512, 16))
    for p in range(k // 512):
        a[p, :8] = np.random.permutation(np.resize(levels, 8))
        for g in range(8):
            far = levels[np.abs(levels - a[p, g]) >= 10]
            a[p, g + 8] = far[np.random.randint(len(far))]
    return np.exp2(a.ravel()).repeat(32)


def f64(x):
    return np.asarray(x).astype(np.float64)


def gelu(v):
    return 0.5 * v * (1.0 + np.tanh(0.7978845608028654 * (v + 0.044715 * v ** 3)))


G, D, M, N = 2, 256, 256, 512


def setup_inputs():
    n = np.random.standard_normal
    s = mx_kscale(D, 0)[:, None]
    return {
        "x": (n((G, D, N)) * s).astype(np.float32),
        "w": (n((G, D, M)) / np.sqrt(D) / s).astype(np.float32),
        "u": (n((G, D, M)) / np.sqrt(D) / s).astype(np.float32),
        "b": (0.5 * n((G, M, 1))).astype(np.float32),
    }


def reference(x, w, u, b):
    xq = mxq(f64(x), 1, "e4m3")
    h = mxq(f64(w), 1, "e4m3").transpose(0, 2, 1) @ xq
    g = mxq(f64(u), 1, "e4m3").transpose(0, 2, 1) @ xq
    h = h + f64(b)
    y = gelu(h) * g
    return y

@@ -1,0 +1,153 @@
+from contextlib import ExitStack
+
+import concourse.mybir as mybir
+
+G, D, M, N = 2, 256, 256, 512
+FLOPS = 2 * 2 * G * D * M * N
+
+F32 = mybir.dt.float32
+BF16 = mybir.dt.bfloat16
+U32 = mybir.dt.uint32
+U8 = mybir.dt.uint8
+FP8X4 = mybir.dt.float8_e4m3fn_x4
+GELU = mybir.ActivationFunctionType.Gelu_apprx_tanh
+
+P = 128
+R = 64
+PACK = 4
+T = 128
+
+LOADS = ["W0","X0","U0","X1","W1","U1","X2","X3"]
+VSHARE = {"W0":128,"X0":80,"U0":128,"X1":128,"W1":0,"U1":32,"X2":64,"X3":128}
+BLOCKS = {"A":[[0],[0],0,0],"B":[[0],[1],0,128],"C":[[1],[0,1],1,0],"D":[[0,1],[2],0,256],"E":[[0,1],[3],1,256]}
+STEPS = ["ilV W0","tr","ilV X0","ilS X0","q W0","q X0","ilV U0","mm W A","q U0","gelu A 0 0","gelu A 1 0","ilV X1","mm U A","ilS W1","q X1","mul A 0 AB","mul A 1 AB","mm W B","ilS U1","q W1","mm U B","ilV U1","mm W C","ilV X2","ilS X2","q U1","gelu B 0 0","gelu B 1 0","q X2","ilV X3","mm U C","gelu C 0 0","gelu C 1 0","mm W D","mul B 0 AB","mul B 1 AB","st AB","q X3","mm U D","mm W E","gelu D 0 0","gelu D 0 1","gelu D 1 0","gelu D 1 1","mul C 0 C","mul C 1 C","st C","mm U E","gelu E 0 0","gelu E 0 1","gelu E 1 0","gelu E 1 1","mul D 0 D","mul D 1 D","st D","mul E 0 E0","st E0","mul E 1 E1","st E1"]
+STORES = {"AB":[[0],[0,1],[0,1]],"C":[[1],[0,1],[0,1]],"D":[[0,1],[2],[0,1]],"E0":[[0,1],[3],[0]],"E1":[[0,1],[3],[1]]}
+
+
+def tile_rows_gglu_gelu_bias_kernel(tc, x, w, u, b, out):
+    nc = tc.nc
+    src = {"X": x, "W": w, "U": u}
+    with ExitStack() as ctx:
+        sb = ctx.enter_context(tc.tile_pool(name="sb", bufs=1))
+        ps = ctx.enter_context(tc.psum_pool(name="ps", bufs=1))
+        ctx.enter_context(tc.manual_schedule())
+
+        brows = sb.tile([P, P], F32, name="brows", align_bytes=64)
+        bcols = sb.tile([P, P], F32, name="bcols", align_bytes=64)
+        warm_in = sb.tile([P, 8], F32, name="warm_in")
+        warm_out = sb.tile([P, 8], F32, name="warm_out")
+        nc.vector.memset(brows[:], 0.0)
+        nc.gpsimd.memset(warm_in[:], 0.0)
+        nc.scalar.dma_start(
+            out=brows[0:P:32, :].rearrange("q (r a) -> q r a", a=32),
+            in_=b.rearrange("g (t q a) o -> q (g t) (a o)", t=2, q=4),
+        )
+        nc.scalar.activation(out=warm_out[:], in_=warm_in[:], func=GELU)
+
+        raw, grouped, codes, scales, where = {}, {}, {}, {}, {}
+        for name in LOADS:
+            tiles = [int(ch) for ch in name[1:]]
+            width = T * len(tiles)
+            raw[name] = sb.tile([P, PACK, width], F32, name="raw" + name)
+            grouped[name] = sb.tile([P, width, PACK], BF16, name="grp" + name, align_bytes=64)
+            codes[name] = sb.tile([P, width], U32, name="cod" + name, align_bytes=64)
+            scales[name] = sb.tile([P, width], U8, name="sca" + name, align_bytes=64)
+            for i, t in enumerate(tiles):
+                where[(name[0], t)] = (name, slice(i * T, (i + 1) * T))
+            view = src[name[0]].rearrange("g (p j) c -> (g p) j c", j=PACK)
+            nc.sync.dma_start(out=raw[name][:], in_=view[:, :, tiles[0] * T : tiles[0] * T + width])
+
+        banks = {}
+        for k in "WU":
+            for g in range(G):
+                for i in range(2):
+                    banks[(k, g, i)] = ps.tile([P, 512], F32, name="bank%s%d%d" % (k, g, i))
+        act, res = {}, {}
+        for blk in BLOCKS:
+            mts, cols, bank, off = BLOCKS[blk]
+            act[blk] = sb.tile([P, G, len(mts) * len(cols) * T], F32, name="act" + blk)
+        for st in STORES:
+            mts, cols, gs = STORES[st]
+            res[st] = sb.tile([P, len(gs), len(mts), len(cols) * T], F32, name="res" + st)
+
+        def il(dst, s, eng):
+            d = dst.rearrange("p (c i) t -> p c t i", i=4)
+            s2 = s.rearrange("p t (c i) -> p c t i", i=4)
+            if eng == "V":
+                nc.vector.tensor_copy(out=d, in_=s2)
+            elif eng == "S":
+                nc.scalar.copy(out=d, in_=s2)
+            else:
+                nc.gpsimd.tensor_scalar(out=d, in0=s2, scalar1=1.0, scalar2=0.0, op0=mybir.AluOpType.mult, op1=mybir.AluOpType.add)
+
+        for step in STEPS:
+            f = step.split(" ")
+            if f[0] == "tr":
+                nc.vector.transpose(out=bcols[:], in_=brows[:])
+            elif f[0] == "ilV":
+                n = VSHARE[f[1]]
+                il(grouped[f[1]][:, 0:n, :], raw[f[1]][:, :, 0:n], "V")
+            elif f[0] == "ilS" or f[0] == "ilG":
+                n = VSHARE[f[1]]
+                il(grouped[f[1]][:, n:, :], raw[f[1]][:, :, n:], f[0][2])
+            elif f[0] == "q":
+                nc.vector.quantize_mx(
+                    out=codes[f[1]][:].bitcast(FP8X4),
+                    scales=scales[f[1]][:],
+                    in_=grouped[f[1]][:].rearrange("p c j -> p (c j)"),
+                )
+            elif f[0] == "mm":
+                k, blk = f[1], f[2]
+                mts, cols, bank, off = BLOCKS[blk]
+                for a, mt in enumerate(mts):
+                    for c, col in enumerate(cols):
+                        wn, wsl = where[(k, mt)]
+                        xn, xsl = where[("X", col)]
+                        o = off + (a * len(cols) + c) * T
+                        for g in range(G):
+                            rows = slice(R * g, R * g + R)
+                            nc.tensor.matmul_mx(
+                                out=banks[(k, g, bank)][:, o : o + T],
+                                lhsT=codes[wn][rows, wsl].bitcast(FP8X4),
+                                lhsT_scale=scales[wn][rows, wsl],
+                                rhs=codes[xn][rows, xsl].bitcast(FP8X4),
+                                rhs_scale=scales[xn][rows, xsl],
+                                start=True,
+                                stop=True,
+                            )
+            elif f[0] == "gelu":
+                blk, g, a = f[1], int(f[2]), int(f[3])
+                mts, cols, bank, off = BLOCKS[blk]
+                wd = len(cols) * T
+                r = 2 * g + mts[a]
+                nc.scalar.activation(
+                    out=act[blk][:, g, a * wd : (a + 1) * wd],
+                    in_=banks[("W", g, bank)][:, off + a * wd : off + (a + 1) * wd],
+                    func=GELU,
+                    bias=bcols[:, 32 * r : 32 * r + 1],
+                )
+            elif f[0] == "mul":
+                blk, g, st = f[1], int(f[2]), f[3]
+                mts, cols, bank, off = BLOCKS[blk]
+                smts, scols, sgs = STORES[st]
+                wd = len(cols) * T
+                sel = list(range(len(mts))) if len(f) == 4 else [int(f[4])]
+                a0, na = sel[0], len(sel)
+                c0 = scols.index(cols[0]) * T
+                m0 = smts.index(mts[a0])
+                nc.vector.tensor_tensor(
+                    out=res[st][:, sgs.index(g), m0 : m0 + na, c0 : c0 + wd],
+                    in0=banks[("U", g, bank)][:, off + a0 * wd : off + (a0 + na) * wd].rearrange("p (a c) -> p a c", a=na),
+                    in1=act[blk][:, g, a0 * wd : (a0 + na) * wd].rearrange("p (a c) -> p a c", a=na),
+                    op=mybir.AluOpType.mult,
+                )
+            else:
+                st = f[1]
+                smts, scols, sgs = STORES[st]
+                view = out.rearrange("g (t p) n -> p g t n", p=P)
+                dst = view[:, sgs[0] : sgs[-1] + 1, smts[0] : smts[-1] + 1, scols[0] * T : (scols[-1] + 1) * T]
+                eng = nc.sync if f[0] == "st" else nc.scalar
+                if len(smts) == 2:
+                    eng.dma_start(out=dst.rearrange("p g t n -> p (g t) n"), in_=res[st][:].rearrange("p g t n -> p (g t) n"))
+                else:
+                    eng.dma_start(out=dst.rearrange("p g t n -> p g (t n)"), in_=res[st][:].rearrange("p g t n -> p g (t n)"))

@@ -17,11 +17,11 @@ R = 64
 PACK = 4
 T = 128
 
-LOADS = ["W0","X0","U0","X1","W1","U1","X2","X3"]
-VSHARE = {"W0":128,"X0":80,"U0":128,"X1":128,"W1":0,"U1":32,"X2":64,"X3":128}
-BLOCKS = {"A":[[0],[0],0,0],"B":[[0],[1],0,128],"C":[[1],[0,1],1,0],"D":[[0,1],[2],0,256],"E":[[0,1],[3],1,256]}
-STEPS = ["ilV W0","tr","ilV X0","ilS X0","q W0","q X0","ilV U0","mm W A","q U0","gelu A 0 0","gelu A 1 0","ilV X1","mm U A","ilS W1","q X1","mul A 0 AB","mul A 1 AB","mm W B","ilS U1","q W1","mm U B","ilV U1","mm W C","ilV X2","ilS X2","q U1","gelu B 0 0","gelu B 1 0","q X2","ilV X3","mm U C","gelu C 0 0","gelu C 1 0","mm W D","mul B 0 AB","mul B 1 AB","st AB","q X3","mm U D","mm W E","gelu D 0 0","gelu D 0 1","gelu D 1 0","gelu D 1 1","mul C 0 C","mul C 1 C","st C","mm U E","gelu E 0 0","gelu E 0 1","gelu E 1 0","gelu E 1 1","mul D 0 D","mul D 1 D","st D","mul E 0 E0","st E0","mul E 1 E1","st E1"]
-STORES = {"AB":[[0],[0,1],[0,1]],"C":[[1],[0,1],[0,1]],"D":[[0,1],[2],[0,1]],"E0":[[0,1],[3],[0]],"E1":[[0,1],[3],[1]]}
+LOADS = ["W0","X01","U0","W1","U1","X2","X3"]
+VSHARE = {"W0":128,"X01":160,"U0":0,"W1":128,"U1":80,"X2":64,"X3":80}
+BLOCKS = {"A":[[0],[0,1],0,0],"C":[[1],[0,1],1,0],"D":[[0,1],[2],0,256],"E":[[0,1],[3],1,256]}
+STEPS = ["ilV W0","q W0","ilV X01","ilS X01","q X01","mm W A","tr","ilS U0","q U0","mm U A","ilV W1","gelu A 0 0","ilV U1","ilS U1","q W1","mm W C","q U1","mm U C","gelu A 1 0","ilV X2","ilS X2","mul A 0 A0","st A0","q X2","mm W D","gelu C 0 0","ilV X3","ilS X3","mul A 1 A1","st A1","mm U D","q X3","gelu C 1 0","mm W E","mul C 0 C0","st C0","mul C 1 C1","st C1","mm U E","gelu D 0 0","gelu D 0 1","gelu D 1 0","gelu D 1 1","mul D 0 D0","st D0","mul D 1 D1","st D1","gelu E 0 0","gelu E 0 1","gelu E 1 0","gelu E 1 1","mul E 0 E0","st E0","mul E 1 E10 0","st E10","mul E 1 E11 1","st E11"]
+STORES = {"A0":[[0],[0,1],[0]],"A1":[[0],[0,1],[1]],"C0":[[1],[0,1],[0]],"C1":[[1],[0,1],[1]],"D0":[[0,1],[2],[0]],"D1":[[0,1],[2],[1]],"E0":[[0,1],[3],[0]],"E10":[[0],[3],[1]],"E11":[[1],[3],[1]]}
 
 
 def tile_rows_gglu_gelu_bias_kernel(tc, x, w, u, b, out):
@@ -37,7 +37,7 @@ def tile_rows_gglu_gelu_bias_kernel(tc, x, w, u, b, out):
         warm_in = sb.tile([P, 8], F32, name="warm_in")
         warm_out = sb.tile([P, 8], F32, name="warm_out")
         nc.vector.memset(brows[:], 0.0)
-        nc.gpsimd.memset(warm_in[:], 0.0)
+        nc.vector.memset(warm_in[:], 0.0)
         nc.scalar.dma_start(
             out=brows[0:P:32, :].rearrange("q (r a) -> q r a", a=32),
             in_=b.rearrange("g (t q a) o -> q (g t) (a o)", t=2, q=4),

from contextlib import ExitStack

import concourse.mybir as mybir

G, D, M, N = 2, 256, 256, 512
FLOPS = 2 * 2 * G * D * M * N

F32 = mybir.dt.float32
BF16 = mybir.dt.bfloat16
U32 = mybir.dt.uint32
U8 = mybir.dt.uint8
FP8X4 = mybir.dt.float8_e4m3fn_x4
GELU = mybir.ActivationFunctionType.Gelu_apprx_tanh

P = 128
R = 64
PACK = 4
T = 128

LOADS = ["W0","X01","U0","W1","U1","X2","X3"]
VSHARE = {"W0":128,"X01":160,"U0":0,"W1":128,"U1":80,"X2":64,"X3":80}
BLOCKS = {"A":[[0],[0,1],0,0],"C":[[1],[0,1],1,0],"D":[[0,1],[2],0,256],"E":[[0,1],[3],1,256]}
STEPS = ["ilV W0","q W0","ilV X01","ilS X01","q X01","mm W A","tr","ilS U0","q U0","mm U A","ilV W1","gelu A 0 0","ilV U1","ilS U1","q W1","mm W C","q U1","mm U C","gelu A 1 0","ilV X2","ilS X2","mul A 0 A0","st A0","q X2","mm W D","gelu C 0 0","ilV X3","ilS X3","mul A 1 A1","st A1","mm U D","q X3","gelu C 1 0","mm W E","mul C 0 C0","st C0","mul C 1 C1","st C1","mm U E","gelu D 0 0","gelu D 0 1","gelu D 1 0","gelu D 1 1","mul D 0 D0","st D0","mul D 1 D1","st D1","gelu E 0 0","gelu E 0 1","gelu E 1 0","gelu E 1 1","mul E 0 E0","st E0","mul E 1 E10 0","st E10","mul E 1 E11 1","st E11"]
STORES = {"A0":[[0],[0,1],[0]],"A1":[[0],[0,1],[1]],"C0":[[1],[0,1],[0]],"C1":[[1],[0,1],[1]],"D0":[[0,1],[2],[0]],"D1":[[0,1],[2],[1]],"E0":[[0,1],[3],[0]],"E10":[[0],[3],[1]],"E11":[[1],[3],[1]]}


def tile_rows_gglu_gelu_bias_kernel(tc, x, w, u, b, out):
    nc = tc.nc
    src = {"X": x, "W": w, "U": u}
    with ExitStack() as ctx:
        sb = ctx.enter_context(tc.tile_pool(name="sb", bufs=1))
        ps = ctx.enter_context(tc.psum_pool(name="ps", bufs=1))
        ctx.enter_context(tc.manual_schedule())

        brows = sb.tile([P, P], F32, name="brows", align_bytes=64)
        bcols = sb.tile([P, P], F32, name="bcols", align_bytes=64)
        warm_in = sb.tile([P, 8], F32, name="warm_in")
        warm_out = sb.tile([P, 8], F32, name="warm_out")
        nc.vector.memset(brows[:], 0.0)
        nc.vector.memset(warm_in[:], 0.0)
        nc.scalar.dma_start(
            out=brows[0:P:32, :].rearrange("q (r a) -> q r a", a=32),
            in_=b.rearrange("g (t q a) o -> q (g t) (a o)", t=2, q=4),
        )
        nc.scalar.activation(out=warm_out[:], in_=warm_in[:], func=GELU)

        raw, grouped, codes, scales, where = {}, {}, {}, {}, {}
        for name in LOADS:
            tiles = [int(ch) for ch in name[1:]]
            width = T * len(tiles)
            raw[name] = sb.tile([P, PACK, width], F32, name="raw" + name)
            grouped[name] = sb.tile([P, width, PACK], BF16, name="grp" + name, align_bytes=64)
            codes[name] = sb.tile([P, width], U32, name="cod" + name, align_bytes=64)
            scales[name] = sb.tile([P, width], U8, name="sca" + name, align_bytes=64)
            for i, t in enumerate(tiles):
                where[(name[0], t)] = (name, slice(i * T, (i + 1) * T))
            view = src[name[0]].rearrange("g (p j) c -> (g p) j c", j=PACK)
            nc.sync.dma_start(out=raw[name][:], in_=view[:, :, tiles[0] * T : tiles[0] * T + width])

        banks = {}
        for k in "WU":
            for g in range(G):
                for i in range(2):
                    banks[(k, g, i)] = ps.tile([P, 512], F32, name="bank%s%d%d" % (k, g, i))
        act, res = {}, {}
        for blk in BLOCKS:
            mts, cols, bank, off = BLOCKS[blk]
            act[blk] = sb.tile([P, G, len(mts) * len(cols) * T], F32, name="act" + blk)
        for st in STORES:
            mts, cols, gs = STORES[st]
            res[st] = sb.tile([P, len(gs), len(mts), len(cols) * T], F32, name="res" + st)

        def il(dst, s, eng):
            d = dst.rearrange("p (c i) t -> p c t i", i=4)
            s2 = s.rearrange("p t (c i) -> p c t i", i=4)
            if eng == "V":
                nc.vector.tensor_copy(out=d, in_=s2)
            elif eng == "S":
                nc.scalar.copy(out=d, in_=s2)
            else:
                nc.gpsimd.tensor_scalar(out=d, in0=s2, scalar1=1.0, scalar2=0.0, op0=mybir.AluOpType.mult, op1=mybir.AluOpType.add)

        for step in STEPS:
            f = step.split(" ")
            if f[0] == "tr":
                nc.vector.transpose(out=bcols[:], in_=brows[:])
            elif f[0] == "ilV":
                n = VSHARE[f[1]]
                il(grouped[f[1]][:, 0:n, :], raw[f[1]][:, :, 0:n], "V")
            elif f[0] == "ilS" or f[0] == "ilG":
                n = VSHARE[f[1]]
                il(grouped[f[1]][:, n:, :], raw[f[1]][:, :, n:], f[0][2])
            elif f[0] == "q":
                nc.vector.quantize_mx(
                    out=codes[f[1]][:].bitcast(FP8X4),
                    scales=scales[f[1]][:],
                    in_=grouped[f[1]][:].rearrange("p c j -> p (c j)"),
                )
            elif f[0] == "mm":
                k, blk = f[1], f[2]
                mts, cols, bank, off = BLOCKS[blk]
                for a, mt in enumerate(mts):
                    for c, col in enumerate(cols):
                        wn, wsl = where[(k, mt)]
                        xn, xsl = where[("X", col)]
                        o = off + (a * len(cols) + c) * T
                        for g in range(G):
                            rows = slice(R * g, R * g + R)
                            nc.tensor.matmul_mx(
                                out=banks[(k, g, bank)][:, o : o + T],
                                lhsT=codes[wn][rows, wsl].bitcast(FP8X4),
                                lhsT_scale=scales[wn][rows, wsl],
                                rhs=codes[xn][rows, xsl].bitcast(FP8X4),
                                rhs_scale=scales[xn][rows, xsl],
                                start=True,
                                stop=True,
                            )
            elif f[0] == "gelu":
                blk, g, a = f[1], int(f[2]), int(f[3])
                mts, cols, bank, off = BLOCKS[blk]
                wd = len(cols) * T
                r = 2 * g + mts[a]
                nc.scalar.activation(
                    out=act[blk][:, g, a * wd : (a + 1) * wd],
                    in_=banks[("W", g, bank)][:, off + a * wd : off + (a + 1) * wd],
                    func=GELU,
                    bias=bcols[:, 32 * r : 32 * r + 1],
                )
            elif f[0] == "mul":
                blk, g, st = f[1], int(f[2]), f[3]
                mts, cols, bank, off = BLOCKS[blk]
                smts, scols, sgs = STORES[st]
                wd = len(cols) * T
                sel = list(range(len(mts))) if len(f) == 4 else [int(f[4])]
                a0, na = sel[0], len(sel)
                c0 = scols.index(cols[0]) * T
                m0 = smts.index(mts[a0])
                nc.vector.tensor_tensor(
                    out=res[st][:, sgs.index(g), m0 : m0 + na, c0 : c0 + wd],
                    in0=banks[("U", g, bank)][:, off + a0 * wd : off + (a0 + na) * wd].rearrange("p (a c) -> p a c", a=na),
                    in1=act[blk][:, g, a0 * wd : (a0 + na) * wd].rearrange("p (a c) -> p a c", a=na),
                    op=mybir.AluOpType.mult,
                )
            else:
                st = f[1]
                smts, scols, sgs = STORES[st]
                view = out.rearrange("g (t p) n -> p g t n", p=P)
                dst = view[:, sgs[0] : sgs[-1] + 1, smts[0] : smts[-1] + 1, scols[0] * T : (scols[-1] + 1) * T]
                eng = nc.sync if f[0] == "st" else nc.scalar
                if len(smts) == 2:
                    eng.dma_start(out=dst.rearrange("p g t n -> p (g t) n"), in_=res[st][:].rearrange("p g t n -> p (g t) n"))
                else:
                    eng.dma_start(out=dst.rearrange("p g t n -> p g (t n)"), in_=res[st][:].rearrange("p g t n -> p g (t n)"))
